import numpy as np
import ml_dtypes


def mxq(x, axis, fmt="e4m3"):
    dtype, down = {"e4m3": (ml_dtypes.float8_e4m3fn, 7), "e5m2": (ml_dtypes.float8_e5m2, 14)}[fmt]
    v = np.moveaxis(np.asarray(x, np.float32).astype(ml_dtypes.bfloat16).astype(np.float64), axis, -1)
    blocks = v.reshape(v.shape[:-1] + (-1, 32))
    amax = np.abs(blocks).max(-1, keepdims=True)
    byte = np.maximum(np.where(amax > 0, np.frexp(amax)[1] - 1 + 127, 0) - down, 1)
    scale = np.exp2(byte - 127.0)
    codes = (blocks / scale).astype(np.float32).astype(dtype).astype(np.float64)
    return np.moveaxis((codes * scale).reshape(v.shape), -1, axis)


WIDE = False


def mx_kscale(k):
    if not WIDE:
        return np.ones(k)
    levels = np.array([10, -10, 5, -5, 0])
    if k % 512:
        return np.exp2(np.random.permutation(np.resize(levels, k // 32))).repeat(32)
    a = np.empty((k // 512, 16))
    for p in range(k // 512):
        a[p, :8] = np.random.permutation(np.resize(levels, 8))
        for g in range(8):
            far = levels[np.abs(levels - a[p, g]) >= 10]
            a[p, g + 8] = far[np.random.randint(len(far))]
    return np.exp2(a.ravel()).repeat(32)


BF16 = ml_dtypes.bfloat16


def bf(x):
    return np.asarray(x, np.float32).astype(BF16)


def f64(x):
    return np.asarray(x).astype(np.float64)


B, H, T, D, A, C = 8, 1, 512, 512, 3, 3


def key_query_conv(s, w):
    n_q, n_k = s.shape[2], s.shape[3]
    n_a, n_c = w.shape[1], w.shape[2]
    top = n_a - 1
    side = n_c // 2
    sp = np.pad(s, ((0, 0), (0, 0), (top, 0), (side, side)))
    z = np.zeros_like(s)
    for a in range(n_a):
        rows = sp[:, :, top - a:top - a + n_q, :]
        for c in range(n_c):
            z = z + w[None, :, a, c, None, None] * rows[:, :, :, c:c + n_k]
    return z


def softmax(z):
    e = np.exp(z - z.max(-1, keepdims=True))
    return e / e.sum(-1, keepdims=True)


def draw0():
    t = mx_kscale(T)
    sign = np.random.choice([-1.0, 1.0], size=(H, A, C))
    return {
        "q": bf(np.random.standard_normal((B, H, T, D))),
        "k": bf(np.random.standard_normal((B, H, T, D))),
        "v": bf(np.random.standard_normal((B, H, T, D)) / t[:, None]),
        "w": bf(sign * np.random.uniform(0.2, 0.6, (H, A, C))),
        "g": bf(np.random.standard_normal((H, T)) * t),
    }


def core(q, k, v, w, g):
    q, k, v, w, g = f64(q), f64(k), f64(v), f64(w), f64(g)
    t, d = q.shape[2], q.shape[3]
    s = q @ k.transpose(0, 1, 3, 2) / np.sqrt(d)
    z = key_query_conv(s, w)
    p = softmax(z)
    m = np.sqrt(t) * p * g[None, :, None, :]
    return mxq(m, 3, "e4m3") @ mxq(v, 2, "e4m3")


def e4m3fn_bytes(y):
    return np.clip(np.asarray(y, np.float64), -448.0, 448.0).astype(np.float32).astype(ml_dtypes.float8_e4m3fn).view(np.uint8)


def e4m3fn_values(b):
    return np.asarray(b, np.uint8).view(ml_dtypes.float8_e4m3fn).astype(np.float64)


def setup_inputs():
    d = draw0()
    x0 = np.asarray(d['v']).astype(np.float64)
    s = (np.max(np.abs(x0), axis=(0, 1, 3), keepdims=True) / 448.0).astype(np.float32)
    out = {}
    for k, v in d.items():
        if k == 'v':
            out['v_bytes'] = e4m3fn_bytes(x0 / s.astype(np.float64))
            out['v_scale'] = s
        else:
            out[k] = v
    return out


def reference(q, k, v_bytes, v_scale, w, g):
    return core(q, k, e4m3fn_values(v_bytes) * v_scale.astype(np.float64), w, g)

@@ -1,0 +1,319 @@
+import math
+from contextlib import ExitStack
+
+import concourse.mybir as mybir
+from concourse.masks import make_identity
+
+B, T, D, E = 8, 512, 512, 512
+P = 128
+NT = 4
+F32 = mybir.dt.float32
+BF16 = mybir.dt.bfloat16
+U32 = mybir.dt.uint32
+U8 = mybir.dt.uint8
+FP8 = mybir.dt.float8_e4m3fn
+FP8X4 = mybir.dt.float8_e4m3fn_x4
+ALU = mybir.AluOpType
+ACT = mybir.ActivationFunctionType
+AX = mybir.AxisListType
+FLOPS = 2 * 2 * B * T * T * D
+LEAD = 4
+RING = 10
+STEPS = B * NT
+
+PLAN = ((1, (('S', 0), ('V', 1), ('V', 2))), (0, (('G', 0), ('V', 1))), (0, (('G', 2),)), (2, (('V', 0),)), (2, (('G', 1),)), (2, (('G', 2),)))
+N_MAPS = len(PLAN)
+
+
+def tile_multitokenkeyqueryconvattention_t_kernel(tc, q, k, v_bytes, v_scale, w, g, out):
+    nc = tc.nc
+    with ExitStack() as ctx:
+        const = ctx.enter_context(tc.tile_pool(name="const", bufs=1))
+        loads = ctx.enter_context(tc.tile_pool(name="loads", bufs=3))
+        work = ctx.enter_context(tc.tile_pool(name="work", bufs=2))
+        ps_tr = ctx.enter_context(tc.psum_pool(name="ps_tr", bufs=2))
+        ps_st = ctx.enter_context(tc.psum_pool(name="ps_st", bufs=2))
+        ps_z = ctx.enter_context(tc.psum_pool(name="ps_z", bufs=2))
+        ps_pv = ctx.enter_context(tc.psum_pool(name="ps_pv", bufs=1))
+        ps_g = ctx.enter_context(tc.psum_pool(name="ps_g", bufs=1))
+
+        raw = {}
+
+        def load(b):
+            q_rows = loads.tile([P, NT, D], BF16, name="q_rows")
+            nc.sync.dma_start(out=q_rows[:], in_=q[b, 0].rearrange("(p r) d -> p r d", r=NT))
+            k_rows = loads.tile([P, NT, D], BF16, name="k_rows")
+            nc.sync.dma_start(out=k_rows[:], in_=k[b, 0].rearrange("(p r) d -> p r d", r=NT))
+            v_raw = loads.tile([P, NT * E], U8, name="v_raw")
+            nc.sync.dma_start(out=v_raw[:], in_=v_bytes[b, 0].rearrange("(p r) e -> p (r e)", r=NT))
+            raw[b] = (q_rows, k_rows, v_raw)
+
+        load(0)
+        w_row = const.tile([P, 9], BF16, name="w_row")
+        nc.sync.dma_start(out=w_row[:], in_=w.rearrange("h a c -> (h a c)").partition_broadcast(P))
+        g_raw = const.tile([P, NT], BF16, name="g_raw")
+        nc.sync.dma_start(out=g_raw[:], in_=g.rearrange("h (p r) -> p (h r)", r=NT))
+        vs = const.tile([P, NT], F32, name="vs")
+        nc.sync.dma_start(out=vs[:], in_=v_scale.rearrange("o h (p r) x -> p (o h r x)", r=NT))
+        load(1)
+
+        dummy = const.tile([P, 1], F32, name="dummy")
+        nc.vector.memset(dummy[:], 0.0)
+        nc.scalar.activation(out=dummy[:], in_=dummy[:], func=ACT.Exp)
+
+        ident = const.tile([P, P], F32, name="ident")
+        make_identity(nc, ident[:])
+        right = const.tile([P, P], F32, name="right")
+        nc.vector.tensor_copy(out=right[:, 1:P], in_=ident[:, 0 : P - 1])
+        nc.vector.tensor_copy(out=right[:, 0:1], in_=ident[:, P - 1 : P])
+        left = const.tile([P, P], F32, name="left")
+        nc.vector.tensor_copy(out=left[:, 0 : P - 1], in_=ident[:, 1:P])
+        nc.vector.tensor_copy(out=left[:, P - 1 : P], in_=ident[:, 0:1])
+
+        wt = const.tile([P, 9], F32, name="wt")
+        nc.vector.tensor_scalar(out=wt[:], in0=w_row[:], scalar1=-1.0 / math.sqrt(D), scalar2=None, op0=ALU.mult)
+        keep = const.tile([P, 2], F32, name="keep")
+        nc.vector.tensor_scalar(out=keep[:, 0:1], in0=ident[:, P - 1 : P], scalar1=-1.0, scalar2=1.0, op0=ALU.mult, op1=ALU.add)
+        nc.vector.tensor_scalar(out=keep[:, 1:2], in0=ident[:, 0:1], scalar1=-1.0, scalar2=1.0, op0=ALU.mult, op1=ALU.add)
+        wt_first = const.tile([P, 9], F32, name="wt_first")
+        nc.vector.tensor_scalar(out=wt_first[:], in0=wt[:], scalar1=keep[:, 0:1], scalar2=None, op0=ALU.mult)
+        wt_last = const.tile([P, 9], F32, name="wt_last")
+        nc.vector.tensor_scalar(out=wt_last[:], in0=wt[:], scalar1=keep[:, 1:2], scalar2=None, op0=ALU.mult)
+
+        g_col = const.tile([P, NT], F32, name="g_col")
+        nc.vector.tensor_scalar(out=g_col[:], in0=g_raw[:], scalar1=math.sqrt(T), scalar2=None, op0=ALU.mult)
+        gain = ps_g.tile([P, T], F32, name="gain")
+        gain_v = gain[:].rearrange("q (u p e) -> q u p e", u=2, e=2)
+        for t in range(NT):
+            nc.tensor.transpose(gain_v[:, t // 2, :, t % 2], g_col[:, t : t + 1].to_broadcast([P, P]), ident[:])
+
+        ring = []
+        for r in range(RING):
+            slot = const.tile([P, N_MAPS, LEAD + T], F32, name=f"ring{r}", align_bytes=64)
+            nc.vector.memset(slot[:, :, 0:LEAD], 0.0)
+            ring.append(slot)
+
+        turned = {}
+        zs = {}
+        ms = {}
+        mx_m = {}
+        vw = {}
+        vi = {}
+        mx_v = {}
+
+        def weight(a, c, t):
+            table = wt
+            if c == 0 and t == NT - 1:
+                table = wt_first
+            if c == 2 and t == 0:
+                table = wt_last
+            i = 3 * a + c
+            return table[:, i : i + 1]
+
+        banks = {}
+        sts = {}
+        flats = {}
+        accs = {}
+        done = set()
+
+        def turn_pe(n):
+            b, j = divmod(n, NT)
+            which, u = divmod(j, 2)
+            words = raw[b][which][:].rearrange("p r d -> p (r d)").bitcast(F32)
+            bank = ps_tr.tile([P, NT * P], F32, name="bank")
+            for r in range(NT):
+                lo = r * (D // 2) + u * P
+                nc.tensor.transpose(bank[:, r * P : (r + 1) * P], words[:, lo : lo + P], ident[:])
+            banks["t", n] = bank
+
+        def turn_copy(n):
+            j = n % NT
+            bank = banks.pop(("t", n))
+            dst = work.tile([P, T], F32, name=f"turned{j}", align_bytes=64)
+            copy = nc.vector.tensor_copy if (n < 0) else nc.scalar.copy
+            if j < 2:
+                copy(out=dst[:].rearrange("p (i r) -> p i r", r=NT), in_=bank[:].rearrange("p (r i) -> p i r", r=NT))
+            else:
+                copy(out=dst[:], in_=bank[:])
+            turned[n] = dst
+
+        def scores(s):
+            b, t = divmod(s, NT)
+            st = ps_st.tile([P, T], F32, name="st")
+            for n in range(4):
+                u, e = divmod(n, 2)
+                kk = turned[NT * b + 2 + u][:].bitcast(BF16)
+                qq = turned[NT * b + u][:].bitcast(BF16)
+                nc.tensor.matmul(st[:], kk[:, 2 * P * t + e : 2 * P * (t + 1) : 2], qq[:, e : 2 * T : 2], start=(n == 0), stop=(n == 3))
+            sts[s] = st
+
+        def flatten(s):
+            flat = work.tile([P, T], F32, name="flat", bufs=3)
+            nc.scalar.copy(out=flat[:], in_=sts[s][:])
+            flats[s] = flat
+
+        def mult(s):
+            b, t = divmod(s, NT)
+            assert s < RING or ("z", (s - RING) // NT * NT + 3) in done
+            slot = ring[s % RING]
+            for m, (c, taps) in enumerate(PLAN):
+                eng, a = taps[0]
+                dst = slot[:, m, LEAD : LEAD + T]
+                if eng == "S":
+                    nc.scalar.activation(out=dst, in_=sts[s][:], func=ACT.Copy, scale=weight(a, c, t))
+                elif eng == "G":
+                    nc.gpsimd.tensor_scalar(out=dst, in0=flats[s][:], scalar1=weight(a, c, t), scalar2=0.0, op0=ALU.mult, op1=ALU.add)
+                elif eng == "V":
+                    nc.vector.tensor_scalar(out=dst, in0=flats[s][:], scalar1=weight(a, c, t), scalar2=None, op0=ALU.mult)
+            done.add(("m", s))
+
+        def vmult(s):
+            b, t = divmod(s, NT)
+            slot = ring[s % RING]
+            for m, (c, taps) in enumerate(PLAN):
+                eng, a = taps[0]
+                dst = slot[:, m, LEAD : LEAD + T]
+                if eng == "W":
+                    nc.vector.tensor_scalar(out=dst, in0=flats[s][:], scalar1=weight(a, c, t), scalar2=None, op0=ALU.mult)
+
+        def accum(s):
+            b, t = divmod(s, NT)
+            slot = ring[s % RING]
+            assert ("m", s) in done
+            for m, (c, taps) in enumerate(PLAN):
+                for eng, a in taps[1:]:
+                    acc = slot[:, m, LEAD + a : LEAD + T]
+                    nc.vector.scalar_tensor_tensor(out=acc, in0=sts[s][:, 0 : T - a], scalar=weight(a, c, t), in1=acc, op0=ALU.mult, op1=ALU.add)
+            done.add(("a", s))
+
+        def stencil(s):
+            b, it = divmod(s, NT)
+            for t in range(NT):
+                assert ("a", NT * b + t) in done
+            z = ps_z.tile([P, T], F32, name="z")
+            n_last = N_MAPS * NT - 1
+            n = 0
+            for m, (c, taps) in enumerate(PLAN):
+                a = 0 if len(taps) > 1 else taps[0][1]
+                for t in range(NT):
+                    src, perm = t + c - 1, ident
+                    if src < 0:
+                        src, perm = NT - 1, right
+                    if src == NT:
+                        src, perm = 0, left
+                    lo = LEAD + P * it - a
+                    nc.tensor.matmul(z[:, P * t : P * (t + 1)], ring[(NT * b + src) % RING][:, m, lo : lo + P], perm[:], start=(n == 0), stop=(n == n_last), is_transpose=True)
+                    n += 1
+            zs[s] = z
+            done.add(("z", s))
+
+        def lowest(s):
+            low = work.tile([P, 1], F32, name="low", bufs=4)
+            nc.vector.tensor_reduce(out=low[:], in_=zs[s][:], axis=AX.X, op=ALU.min)
+            zs[s] = (zs[s], low)
+
+        def exps(s):
+            z, low = zs[s]
+            e = work.tile([P, T], F32, name="e", bufs=2)
+            total = work.tile([P, 1], F32, name="total", bufs=4)
+            nc.scalar.activation(out=e[:].rearrange("q (u p e) -> q u p e", u=2, e=2), in_=z[:].rearrange("q (u e p) -> q u p e", u=2, e=2), func=ACT.Exp, scale=-1.0, bias=low[:], accum_out=total[:])
+            zs[s] = (e, total, 0)
+
+        def weigh(s):
+            e, total, spare = zs.pop(s)
+            inv = work.tile([P, 1], F32, name="inv", bufs=4)
+            nc.vector.reciprocal(out=inv[:], in_=total[:])
+            m = work.tile([P, T], BF16, name="m", bufs=4)
+            nc.vector.scalar_tensor_tensor(out=m[:], in0=e[:], scalar=inv[:], in1=gain[:], op0=ALU.mult, op1=ALU.mult)
+            ms[s] = m
+
+        def pack_pe(s):
+            if s % 2 == 0:
+                return
+            bank = ps_tr.tile([P, NT * P], F32, name="bank")
+            for i, n in enumerate((s - 1, s)):
+                words = ms.pop(n)[:].bitcast(F32)
+                for u in range(2):
+                    nc.tensor.transpose(bank[:, (2 * i + u) * P : (2 * i + u + 1) * P], words[:, u * P : (u + 1) * P], ident[:])
+            banks["p", s] = bank
+
+        def pack_copy(s):
+            if s % 2 == 0:
+                return
+            bank = banks.pop(("p", s))
+            mt = work.tile([P, 2 * P * NT], BF16, name="mt", align_bytes=64)
+            copy = nc.vector.tensor_copy if 0 else nc.scalar.copy
+            copy(out=mt[:].bitcast(F32).rearrange("p (n i u) -> p n i u", n=2, u=2), in_=bank[:].rearrange("p (n u i) -> p n i u", n=2, u=2))
+            banks["m", s] = mt
+
+        def pack_quant(s):
+            if s % 2 == 0:
+                return
+            mt = banks.pop(("m", s))
+            codes = work.tile([P, 2 * P], U32, name="m_codes", align_bytes=64)
+            scl = work.tile([P, 2 * P], U8, name="m_scl", align_bytes=64)
+            nc.vector.quantize_mx(out=codes[:].bitcast(FP8X4), scales=scl[:], in_=mt[:])
+            for i, n in enumerate((s - 1, s)):
+                mx_m[n] = (codes[:, i * P : (i + 1) * P], scl[:, i * P : (i + 1) * P])
+
+        def widen(s):
+            b, t = divmod(s, NT)
+            if t == 0:
+                v_wide = work.tile([P, NT, E], BF16, name="v_wide")
+                vw[b] = v_wide
+            code = raw[b][2][:, t * E : (t + 1) * E].bitcast(FP8)
+            if 'S' == "S":
+                nc.scalar.activation(out=vw[b][:, t, :], in_=code, func=ACT.Copy, scale=vs[:, t : t + 1])
+            else:
+                nc.vector.tensor_scalar(out=vw[b][:, t, :], in0=code, scalar1=vs[:, t : t + 1], scalar2=None, op0=ALU.mult)
+            done.add(("w", s))
+
+        def interleave(s):
+            b, h = divmod(s, NT)
+            assert ("w", NT * b + 3) in done
+            if h == 0:
+                v_inter = work.tile([P, E, NT], BF16, name="v_inter", align_bytes=64)
+                vi[b] = v_inter
+            cols = slice(h * P, (h + 1) * P)
+            if 'G' == "G":
+                nc.gpsimd.tensor_scalar(out=vi[b][:, cols, :], in0=vw[b][:, :, cols].rearrange("p t n -> p n t"), scalar1=1.0, scalar2=0.0, op0=ALU.mult, op1=ALU.add)
+            else:
+                nc.vector.tensor_copy(out=vi[b][:, cols, :], in_=vw[b][:, :, cols].rearrange("p t n -> p n t"))
+            done.add(("i", s))
+
+        def quant_v(s):
+            b, h = divmod(s, NT)
+            if h != NT - 1:
+                return
+            assert ("i", s) in done
+            codes = work.tile([P, E], U32, name="v_codes", align_bytes=64)
+            scl = work.tile([P, E], U8, name="v_scl", align_bytes=64)
+            nc.vector.quantize_mx(out=codes[:].bitcast(FP8X4), scales=scl[:], in_=vi[b][:].rearrange("p n t -> p (n t)"))
+            mx_v[b] = (codes, scl)
+
+        def product(s):
+            b, it = divmod(s, NT)
+            codes, scl = mx_m.pop(s)
+            vc, vsc = mx_v[b]
+            acc = ps_pv.tile([P, E], F32, name="acc")
+            nc.tensor.matmul_mx(out=acc[:], lhsT=codes.bitcast(FP8X4), lhsT_scale=scl, rhs=vc[:].bitcast(FP8X4), rhs_scale=vsc[:], start=True, stop=True)
+            accs[s] = acc
+
+        def leave(s):
+            b, it = divmod(s, NT)
+            acc = accs.pop(s)
+            res = work.tile([P, E], F32, name="res", bufs=4)
+            copy = nc.vector.tensor_copy if s >= 99 else nc.scalar.copy
+            copy(out=res[:], in_=acc[:])
+            nc.sync.dma_start(out=out[b, 0, it * P : (it + 1) * P, :], in_=res[:])
+
+        def load_(s):
+            if s % NT == 0 and s >= 2 * NT:
+                load(s // NT)
+
+        step = ((stencil, 5), (load_, -8), (lowest, 5), (exps, 5), (pack_pe, 6), (accum, 1), (weigh, 5), (scores, 0), (interleave, 3), (turn_pe, -5), (flatten, 0), (pack_copy, 6), (product, 8), (pack_quant, 6), (widen, -1), (mult, 0), (leave, 8), (quant_v, 3), (turn_copy, -5),)
+        with tc.manual_schedule():
+            for s in range(-8, STEPS + 8 + 1):
+                for fn, lag in step:
+                    if 0 <= s - lag < STEPS:
+                        fn(s - lag)

@@ -18,10 +18,10 @@ ACT = mybir.ActivationFunctionType
 AX = mybir.AxisListType
 FLOPS = 2 * 2 * B * T * T * D
 LEAD = 4
-RING = 10
+RING = 9
 STEPS = B * NT
 
-PLAN = ((1, (('S', 0), ('V', 1), ('V', 2))), (0, (('G', 0), ('V', 1))), (0, (('G', 2),)), (2, (('V', 0),)), (2, (('G', 1),)), (2, (('G', 2),)))
+PLAN = ((1, (('S', 0), ('V', 1), ('V', 2))), (0, (('G', 0),)), (0, (('V', 1),)), (0, (('V', 2),)), (2, (('V', 0),)), (2, (('V', 1),)), (2, (('G', 2),)))
 N_MAPS = len(PLAN)
 
 
@@ -48,12 +48,12 @@ def tile_multitokenkeyqueryconvattention_t_kernel(tc, q, k, v_bytes, v_scale, w,
             nc.sync.dma_start(out=v_raw[:], in_=v_bytes[b, 0].rearrange("(p r) e -> p (r e)", r=NT))
             raw[b] = (q_rows, k_rows, v_raw)
 
-        load(0)
         w_row = const.tile([P, 9], BF16, name="w_row")
         nc.sync.dma_start(out=w_row[:], in_=w.rearrange("h a c -> (h a c)").partition_broadcast(P))
         g_raw = const.tile([P, NT], BF16, name="g_raw")
-        nc.sync.dma_start(out=g_raw[:], in_=g.rearrange("h (p r) -> p (h r)", r=NT))
         vs = const.tile([P, NT], F32, name="vs")
+        load(0)
+        nc.sync.dma_start(out=g_raw[:], in_=g.rearrange("h (p r) -> p (h r)", r=NT))
         nc.sync.dma_start(out=vs[:], in_=v_scale.rearrange("o h (p r) x -> p (o h r x)", r=NT))
         load(1)
 
@@ -83,9 +83,6 @@ def tile_multitokenkeyqueryconvattention_t_kernel(tc, q, k, v_bytes, v_scale, w,
         g_col = const.tile([P, NT], F32, name="g_col")
         nc.vector.tensor_scalar(out=g_col[:], in0=g_raw[:], scalar1=math.sqrt(T), scalar2=None, op0=ALU.mult)
         gain = ps_g.tile([P, T], F32, name="gain")
-        gain_v = gain[:].rearrange("q (u p e) -> q u p e", u=2, e=2)
-        for t in range(NT):
-            nc.tensor.transpose(gain_v[:, t // 2, :, t % 2], g_col[:, t : t + 1].to_broadcast([P, P]), ident[:])
 
         ring = []
         for r in range(RING):
@@ -180,8 +177,8 @@ def tile_multitokenkeyqueryconvattention_t_kernel(tc, q, k, v_bytes, v_scale, w,
             b, t = divmod(s, NT)
             slot = ring[s % RING]
             assert ("m", s) in done
-            for m, (c, taps) in enumerate(PLAN):
-                for eng, a in taps[1:]:
+            todo = [(i, m, c, a) for m, (c, taps) in enumerate(PLAN) for i, (eng, a) in enumerate(taps) if i]
+            for i, m, c, a in sorted(todo):
                     acc = slot[:, m, LEAD + a : LEAD + T]
                     nc.vector.scalar_tensor_tensor(out=acc, in0=sts[s][:, 0 : T - a], scalar=weight(a, c, t), in1=acc, op0=ALU.mult, op1=ALU.add)
             done.add(("a", s))
@@ -219,10 +216,14 @@ def tile_multitokenkeyqueryconvattention_t_kernel(tc, q, k, v_bytes, v_scale, w,
             nc.scalar.activation(out=e[:].rearrange("q (u p e) -> q u p e", u=2, e=2), in_=z[:].rearrange("q (u e p) -> q u p e", u=2, e=2), func=ACT.Exp, scale=-1.0, bias=low[:], accum_out=total[:])
             zs[s] = (e, total, 0)
 
-        def weigh(s):
-            e, total, spare = zs.pop(s)
+        def invert(s):
+            e, total, spare = zs[s]
             inv = work.tile([P, 1], F32, name="inv", bufs=4)
             nc.vector.reciprocal(out=inv[:], in_=total[:])
+            zs[s] = (e, inv, 0, 0)
+
+        def weigh(s):
+            e, inv, spare, spare = zs.pop(s)
             m = work.tile([P, T], BF16, name="m", bufs=4)
             nc.vector.scalar_tensor_tensor(out=m[:], in0=e[:], scalar=inv[:], in1=gain[:], op0=ALU.mult, op1=ALU.mult)
             ms[s] = m
@@ -311,9 +312,16 @@ def tile_multitokenkeyqueryconvattention_t_kernel(tc, q, k, v_bytes, v_scale, w,
             if s % NT == 0 and s >= 2 * NT:
                 load(s // NT)
 
-        step = ((stencil, 5), (load_, -8), (lowest, 5), (exps, 5), (pack_pe, 6), (accum, 1), (weigh, 5), (scores, 0), (interleave, 3), (turn_pe, -5), (flatten, 0), (pack_copy, 6), (product, 8), (pack_quant, 6), (widen, -1), (mult, 0), (leave, 8), (quant_v, 3), (turn_copy, -5),)
+        def spread(s):
+            if s:
+                return
+            gain_v = gain[:].rearrange("q (u p e) -> q u p e", u=2, e=2)
+            for t in range(NT):
+                nc.tensor.transpose(gain_v[:, t // 2, :, t % 2], g_col[:, t : t + 1].to_broadcast([P, P]), ident[:])
+
+        step = ((load_, -8), (stencil, 5), (scores, 0), (exps, 6), (accum, 1), (leave, 10), (flatten, 0), (spread, 0), (invert, 6), (lowest, 5), (quant_v, 5), (weigh, 6), (pack_pe, 7), (turn_pe, -5), (pack_copy, 7), (pack_quant, 7), (mult, 0), (widen, 0), (turn_copy, -5), (interleave, 3), (product, 9),)
         with tc.manual_schedule():
-            for s in range(-8, STEPS + 8 + 1):
+            for s in range(-8, STEPS + 10 + 1):
                 for fn, lag in step:
                     if 0 <= s - lag < STEPS:
                         fn(s - lag)

@@ -21,7 +21,7 @@ LEAD = 4
 RING = 9
 STEPS = B * NT
 
-PLAN = ((1, (('S', 0), ('V', 1), ('V', 2))), (0, (('G', 0),)), (0, (('V', 1),)), (0, (('V', 2),)), (2, (('V', 0),)), (2, (('V', 1),)), (2, (('G', 2),)))
+PLAN = ((1, (('S', 0), ('V', 1), ('V', 2),)), (0, (('X', 0),)), (0, (('G', 1),)), (0, (('V', 2),)), (2, (('V', 0),)), (2, (('V', 1),)), (2, (('V', 2),)))
 N_MAPS = len(PLAN)
 
 
@@ -81,7 +81,6 @@ def tile_multitokenkeyqueryconvattention_t_kernel(tc, q, k, v_bytes, v_scale, w,
         nc.vector.tensor_scalar(out=wt_last[:], in0=wt[:], scalar1=keep[:, 1:2], scalar2=None, op0=ALU.mult)
 
         g_col = const.tile([P, NT], F32, name="g_col")
-        nc.vector.tensor_scalar(out=g_col[:], in0=g_raw[:], scalar1=math.sqrt(T), scalar2=None, op0=ALU.mult)
         gain = ps_g.tile([P, T], F32, name="gain")
 
         ring = []
@@ -127,7 +126,7 @@ def tile_multitokenkeyqueryconvattention_t_kernel(tc, q, k, v_bytes, v_scale, w,
             j = n % NT
             bank = banks.pop(("t", n))
             dst = work.tile([P, T], F32, name=f"turned{j}", align_bytes=64)
-            copy = nc.vector.tensor_copy if (n < 0) else nc.scalar.copy
+            copy = nc.vector.tensor_copy if (n < 0 and n % 2) else nc.scalar.copy
             if j < 2:
                 copy(out=dst[:].rearrange("p (i r) -> p i r", r=NT), in_=bank[:].rearrange("p (r i) -> p i r", r=NT))
             else:
@@ -145,7 +144,7 @@ def tile_multitokenkeyqueryconvattention_t_kernel(tc, q, k, v_bytes, v_scale, w,
             sts[s] = st
 
         def flatten(s):
-            flat = work.tile([P, T], F32, name="flat", bufs=3)
+            flat = work.tile([P, T], F32, name="flat", bufs=2)
             nc.scalar.copy(out=flat[:], in_=sts[s][:])
             flats[s] = flat
 
@@ -155,6 +154,10 @@ def tile_multitokenkeyqueryconvattention_t_kernel(tc, q, k, v_bytes, v_scale, w,
             slot = ring[s % RING]
             for m, (c, taps) in enumerate(PLAN):
                 eng, a = taps[0]
+                if eng == "X":
+                    eng = "SV"[t % 2]
+                if eng == "Y":
+                    eng = "GV"[t % 2]
                 dst = slot[:, m, LEAD : LEAD + T]
                 if eng == "S":
                     nc.scalar.activation(out=dst, in_=sts[s][:], func=ACT.Copy, scale=weight(a, c, t))
@@ -228,33 +231,40 @@ def tile_multitokenkeyqueryconvattention_t_kernel(tc, q, k, v_bytes, v_scale, w,
             nc.vector.scalar_tensor_tensor(out=m[:], in0=e[:], scalar=inv[:], in1=gain[:], op0=ALU.mult, op1=ALU.mult)
             ms[s] = m
 
+        def group(s):
+            if s >= 30:
+                return (s,)
+            return (s - 1, s) if s % 2 else ()
+
         def pack_pe(s):
-            if s % 2 == 0:
+            if not group(s):
                 return
             bank = ps_tr.tile([P, NT * P], F32, name="bank")
-            for i, n in enumerate((s - 1, s)):
+            for i, n in enumerate(group(s)):
                 words = ms.pop(n)[:].bitcast(F32)
                 for u in range(2):
                     nc.tensor.transpose(bank[:, (2 * i + u) * P : (2 * i + u + 1) * P], words[:, u * P : (u + 1) * P], ident[:])
             banks["p", s] = bank
 
         def pack_copy(s):
-            if s % 2 == 0:
+            if not group(s):
                 return
             bank = banks.pop(("p", s))
+            w = len(group(s)) * P
             mt = work.tile([P, 2 * P * NT], BF16, name="mt", align_bytes=64)
             copy = nc.vector.tensor_copy if 0 else nc.scalar.copy
-            copy(out=mt[:].bitcast(F32).rearrange("p (n i u) -> p n i u", n=2, u=2), in_=bank[:].rearrange("p (n u i) -> p n i u", n=2, u=2))
+            copy(out=mt[:, 0 : NT * w].bitcast(F32).rearrange("p (n i u) -> p n i u", i=P, u=2), in_=bank[:, 0 : 2 * w].rearrange("p (n u i) -> p n i u", i=P, u=2))
             banks["m", s] = mt
 
         def pack_quant(s):
-            if s % 2 == 0:
+            if not group(s):
                 return
             mt = banks.pop(("m", s))
-            codes = work.tile([P, 2 * P], U32, name="m_codes", align_bytes=64)
-            scl = work.tile([P, 2 * P], U8, name="m_scl", align_bytes=64)
-            nc.vector.quantize_mx(out=codes[:].bitcast(FP8X4), scales=scl[:], in_=mt[:])
-            for i, n in enumerate((s - 1, s)):
+            w = len(group(s)) * P
+            codes = work.tile([P, 2 * P], U32, name="m_codes", align_bytes=64, bufs=3)
+            scl = work.tile([P, 2 * P], U8, name="m_scl", align_bytes=64, bufs=3)
+            nc.vector.quantize_mx(out=codes[:, 0:w].bitcast(FP8X4), scales=scl[:, 0:w], in_=mt[:, 0 : NT * w])
+            for i, n in enumerate(group(s)):
                 mx_m[n] = (codes[:, i * P : (i + 1) * P], scl[:, i * P : (i + 1) * P])
 
         def widen(s):
@@ -296,7 +306,10 @@ def tile_multitokenkeyqueryconvattention_t_kernel(tc, q, k, v_bytes, v_scale, w,
             b, it = divmod(s, NT)
             codes, scl = mx_m.pop(s)
             vc, vsc = mx_v[b]
-            acc = ps_pv.tile([P, E], F32, name="acc")
+            if s >= 28 and s % 2:
+                acc = ps_st.tile([P, E], F32, name="st")
+            else:
+                acc = ps_pv.tile([P, E], F32, name="acc")
             nc.tensor.matmul_mx(out=acc[:], lhsT=codes.bitcast(FP8X4), lhsT_scale=scl, rhs=vc[:].bitcast(FP8X4), rhs_scale=vsc[:], start=True, stop=True)
             accs[s] = acc
 
@@ -304,9 +317,13 @@ def tile_multitokenkeyqueryconvattention_t_kernel(tc, q, k, v_bytes, v_scale, w,
             b, it = divmod(s, NT)
             acc = accs.pop(s)
             res = work.tile([P, E], F32, name="res", bufs=4)
-            copy = nc.vector.tensor_copy if s >= 99 else nc.scalar.copy
+            copy = nc.vector.tensor_copy if s in (29, 31) else nc.scalar.copy
             copy(out=res[:], in_=acc[:])
             nc.sync.dma_start(out=out[b, 0, it * P : (it + 1) * P, :], in_=res[:])
+
+        def finish(s):
+            product(s)
+            leave(s)
 
         def load_(s):
             if s % NT == 0 and s >= 2 * NT:
@@ -315,13 +332,17 @@ def tile_multitokenkeyqueryconvattention_t_kernel(tc, q, k, v_bytes, v_scale, w,
         def spread(s):
             if s:
                 return
+            nc.vector.tensor_scalar(out=g_col[:], in0=g_raw[:], scalar1=math.sqrt(T), scalar2=None, op0=ALU.mult)
             gain_v = gain[:].rearrange("q (u p e) -> q u p e", u=2, e=2)
             for t in range(NT):
                 nc.tensor.transpose(gain_v[:, t // 2, :, t % 2], g_col[:, t : t + 1].to_broadcast([P, P]), ident[:])
 
-        step = ((load_, -8), (stencil, 5), (scores, 0), (exps, 6), (accum, 1), (leave, 10), (flatten, 0), (spread, 0), (invert, 6), (lowest, 5), (quant_v, 5), (weigh, 6), (pack_pe, 7), (turn_pe, -5), (pack_copy, 7), (pack_quant, 7), (mult, 0), (widen, 0), (turn_copy, -5), (interleave, 3), (product, 9),)
+        step = ((exps, 6), (scores, 0), (invert, 6), (spread, -1), (flatten, 0), (pack_pe, 7), (accum, 1), (interleave, 5), (stencil, 5), (widen, 1), (weigh, 6), (turn_pe, -5), (lowest, 5), (mult, 0), (pack_copy, 7), (turn_copy, -5), (quant_v, 5), (product, 9), (pack_quant, 7), (load_, -8), (leave, 9),)
+        tail = ((exps, 6), (scores, 0), (invert, 6), (spread, -2), (flatten, 0), (pack_pe, 7), (accum, 2), (interleave, 5), (stencil, 4), (widen, 1), (weigh, 6), (leave, 10), (lowest, 5), (turn_pe, -4), (mult, 0), (load_, -8), (pack_copy, 7), (turn_copy, -5), (quant_v, 5), (product, 9), (pack_quant, 7),)
+        count = {}
         with tc.manual_schedule():
-            for s in range(-8, STEPS + 10 + 1):
-                for fn, lag in step:
-                    if 0 <= s - lag < STEPS:
-                        fn(s - lag)
+            for s in range(-8, STEPS + 9 + 1):
+                for fn, lag in (tail if s >= 33 else step):
+                    while count.setdefault(fn, count[leave] if fn is finish else 0) <= s - lag and count[fn] < STEPS:
+                        fn(count[fn])
+                        count[fn] += 1

import math
from contextlib import ExitStack

import concourse.mybir as mybir
from concourse.masks import make_identity

B, T, D, E = 8, 512, 512, 512
P = 128
NT = 4
F32 = mybir.dt.float32
BF16 = mybir.dt.bfloat16
U32 = mybir.dt.uint32
U8 = mybir.dt.uint8
FP8 = mybir.dt.float8_e4m3fn
FP8X4 = mybir.dt.float8_e4m3fn_x4
ALU = mybir.AluOpType
ACT = mybir.ActivationFunctionType
AX = mybir.AxisListType
FLOPS = 2 * 2 * B * T * T * D
LEAD = 4
RING = 9
STEPS = B * NT

PLAN = ((1, (('S', 0), ('V', 1), ('V', 2),)), (0, (('X', 0),)), (0, (('G', 1),)), (0, (('V', 2),)), (2, (('V', 0),)), (2, (('V', 1),)), (2, (('V', 2),)))
N_MAPS = len(PLAN)


def tile_multitokenkeyqueryconvattention_t_kernel(tc, q, k, v_bytes, v_scale, w, g, out):
    nc = tc.nc
    with ExitStack() as ctx:
        const = ctx.enter_context(tc.tile_pool(name="const", bufs=1))
        loads = ctx.enter_context(tc.tile_pool(name="loads", bufs=3))
        work = ctx.enter_context(tc.tile_pool(name="work", bufs=2))
        ps_tr = ctx.enter_context(tc.psum_pool(name="ps_tr", bufs=2))
        ps_st = ctx.enter_context(tc.psum_pool(name="ps_st", bufs=2))
        ps_z = ctx.enter_context(tc.psum_pool(name="ps_z", bufs=2))
        ps_pv = ctx.enter_context(tc.psum_pool(name="ps_pv", bufs=1))
        ps_g = ctx.enter_context(tc.psum_pool(name="ps_g", bufs=1))

        raw = {}

        def load(b):
            q_rows = loads.tile([P, NT, D], BF16, name="q_rows")
            nc.sync.dma_start(out=q_rows[:], in_=q[b, 0].rearrange("(p r) d -> p r d", r=NT))
            k_rows = loads.tile([P, NT, D], BF16, name="k_rows")
            nc.sync.dma_start(out=k_rows[:], in_=k[b, 0].rearrange("(p r) d -> p r d", r=NT))
            v_raw = loads.tile([P, NT * E], U8, name="v_raw")
            nc.sync.dma_start(out=v_raw[:], in_=v_bytes[b, 0].rearrange("(p r) e -> p (r e)", r=NT))
            raw[b] = (q_rows, k_rows, v_raw)

        w_row = const.tile([P, 9], BF16, name="w_row")
        nc.sync.dma_start(out=w_row[:], in_=w.rearrange("h a c -> (h a c)").partition_broadcast(P))
        g_raw = const.tile([P, NT], BF16, name="g_raw")
        vs = const.tile([P, NT], F32, name="vs")
        load(0)
        nc.sync.dma_start(out=g_raw[:], in_=g.rearrange("h (p r) -> p (h r)", r=NT))
        nc.sync.dma_start(out=vs[:], in_=v_scale.rearrange("o h (p r) x -> p (o h r x)", r=NT))
        load(1)

        dummy = const.tile([P, 1], F32, name="dummy")
        nc.vector.memset(dummy[:], 0.0)
        nc.scalar.activation(out=dummy[:], in_=dummy[:], func=ACT.Exp)

        ident = const.tile([P, P], F32, name="ident")
        make_identity(nc, ident[:])
        right = const.tile([P, P], F32, name="right")
        nc.vector.tensor_copy(out=right[:, 1:P], in_=ident[:, 0 : P - 1])
        nc.vector.tensor_copy(out=right[:, 0:1], in_=ident[:, P - 1 : P])
        left = const.tile([P, P], F32, name="left")
        nc.vector.tensor_copy(out=left[:, 0 : P - 1], in_=ident[:, 1:P])
        nc.vector.tensor_copy(out=left[:, P - 1 : P], in_=ident[:, 0:1])

        wt = const.tile([P, 9], F32, name="wt")
        nc.vector.tensor_scalar(out=wt[:], in0=w_row[:], scalar1=-1.0 / math.sqrt(D), scalar2=None, op0=ALU.mult)
        keep = const.tile([P, 2], F32, name="keep")
        nc.vector.tensor_scalar(out=keep[:, 0:1], in0=ident[:, P - 1 : P], scalar1=-1.0, scalar2=1.0, op0=ALU.mult, op1=ALU.add)
        nc.vector.tensor_scalar(out=keep[:, 1:2], in0=ident[:, 0:1], scalar1=-1.0, scalar2=1.0, op0=ALU.mult, op1=ALU.add)
        wt_first = const.tile([P, 9], F32, name="wt_first")
        nc.vector.tensor_scalar(out=wt_first[:], in0=wt[:], scalar1=keep[:, 0:1], scalar2=None, op0=ALU.mult)
        wt_last = const.tile([P, 9], F32, name="wt_last")
        nc.vector.tensor_scalar(out=wt_last[:], in0=wt[:], scalar1=keep[:, 1:2], scalar2=None, op0=ALU.mult)

        g_col = const.tile([P, NT], F32, name="g_col")
        gain = ps_g.tile([P, T], F32, name="gain")

        ring = []
        for r in range(RING):
            slot = const.tile([P, N_MAPS, LEAD + T], F32, name=f"ring{r}", align_bytes=64)
            nc.vector.memset(slot[:, :, 0:LEAD], 0.0)
            ring.append(slot)

        turned = {}
        zs = {}
        ms = {}
        mx_m = {}
        vw = {}
        vi = {}
        mx_v = {}

        def weight(a, c, t):
            table = wt
            if c == 0 and t == NT - 1:
                table = wt_first
            if c == 2 and t == 0:
                table = wt_last
            i = 3 * a + c
            return table[:, i : i + 1]

        banks = {}
        sts = {}
        flats = {}
        accs = {}
        done = set()

        def turn_pe(n):
            b, j = divmod(n, NT)
            which, u = divmod(j, 2)
            words = raw[b][which][:].rearrange("p r d -> p (r d)").bitcast(F32)
            bank = ps_tr.tile([P, NT * P], F32, name="bank")
            for r in range(NT):
                lo = r * (D // 2) + u * P
                nc.tensor.transpose(bank[:, r * P : (r + 1) * P], words[:, lo : lo + P], ident[:])
            banks["t", n] = bank

        def turn_copy(n):
            j = n % NT
            bank = banks.pop(("t", n))
            dst = work.tile([P, T], F32, name=f"turned{j}", align_bytes=64)
            copy = nc.vector.tensor_copy if (n < 0 and n % 2) else nc.scalar.copy
            if j < 2:
                copy(out=dst[:].rearrange("p (i r) -> p i r", r=NT), in_=bank[:].rearrange("p (r i) -> p i r", r=NT))
            else:
                copy(out=dst[:], in_=bank[:])
            turned[n] = dst

        def scores(s):
            b, t = divmod(s, NT)
            st = ps_st.tile([P, T], F32, name="st")
            for n in range(4):
                u, e = divmod(n, 2)
                kk = turned[NT * b + 2 + u][:].bitcast(BF16)
                qq = turned[NT * b + u][:].bitcast(BF16)
                nc.tensor.matmul(st[:], kk[:, 2 * P * t + e : 2 * P * (t + 1) : 2], qq[:, e : 2 * T : 2], start=(n == 0), stop=(n == 3))
            sts[s] = st

        def flatten(s):
            flat = work.tile([P, T], F32, name="flat", bufs=2)
            nc.scalar.copy(out=flat[:], in_=sts[s][:])
            flats[s] = flat

        def mult(s):
            b, t = divmod(s, NT)
            assert s < RING or ("z", (s - RING) // NT * NT + 3) in done
            slot = ring[s % RING]
            for m, (c, taps) in enumerate(PLAN):
                eng, a = taps[0]
                if eng == "X":
                    eng = "SV"[t % 2]
                if eng == "Y":
                    eng = "GV"[t % 2]
                dst = slot[:, m, LEAD : LEAD + T]
                if eng == "S":
                    nc.scalar.activation(out=dst, in_=sts[s][:], func=ACT.Copy, scale=weight(a, c, t))
                elif eng == "G":
                    nc.gpsimd.tensor_scalar(out=dst, in0=flats[s][:], scalar1=weight(a, c, t), scalar2=0.0, op0=ALU.mult, op1=ALU.add)
                elif eng == "V":
                    nc.vector.tensor_scalar(out=dst, in0=flats[s][:], scalar1=weight(a, c, t), scalar2=None, op0=ALU.mult)
            done.add(("m", s))

        def vmult(s):
            b, t = divmod(s, NT)
            slot = ring[s % RING]
            for m, (c, taps) in enumerate(PLAN):
                eng, a = taps[0]
                dst = slot[:, m, LEAD : LEAD + T]
                if eng == "W":
                    nc.vector.tensor_scalar(out=dst, in0=flats[s][:], scalar1=weight(a, c, t), scalar2=None, op0=ALU.mult)

        def accum(s):
            b, t = divmod(s, NT)
            slot = ring[s % RING]
            assert ("m", s) in done
            todo = [(i, m, c, a) for m, (c, taps) in enumerate(PLAN) for i, (eng, a) in enumerate(taps) if i]
            for i, m, c, a in sorted(todo):
                    acc = slot[:, m, LEAD + a : LEAD + T]
                    nc.vector.scalar_tensor_tensor(out=acc, in0=sts[s][:, 0 : T - a], scalar=weight(a, c, t), in1=acc, op0=ALU.mult, op1=ALU.add)
            done.add(("a", s))

        def stencil(s):
            b, it = divmod(s, NT)
            for t in range(NT):
                assert ("a", NT * b + t) in done
            z = ps_z.tile([P, T], F32, name="z")
            n_last = N_MAPS * NT - 1
            n = 0
            for m, (c, taps) in enumerate(PLAN):
                a = 0 if len(taps) > 1 else taps[0][1]
                for t in range(NT):
                    src, perm = t + c - 1, ident
                    if src < 0:
                        src, perm = NT - 1, right
                    if src == NT:
                        src, perm = 0, left
                    lo = LEAD + P * it - a
                    nc.tensor.matmul(z[:, P * t : P * (t + 1)], ring[(NT * b + src) % RING][:, m, lo : lo + P], perm[:], start=(n == 0), stop=(n == n_last), is_transpose=True)
                    n += 1
            zs[s] = z
            done.add(("z", s))

        def lowest(s):
            low = work.tile([P, 1], F32, name="low", bufs=4)
            nc.vector.tensor_reduce(out=low[:], in_=zs[s][:], axis=AX.X, op=ALU.min)
            zs[s] = (zs[s], low)

        def exps(s):
            z, low = zs[s]
            e = work.tile([P, T], F32, name="e", bufs=2)
            total = work.tile([P, 1], F32, name="total", bufs=4)
            nc.scalar.activation(out=e[:].rearrange("q (u p e) -> q u p e", u=2, e=2), in_=z[:].rearrange("q (u e p) -> q u p e", u=2, e=2), func=ACT.Exp, scale=-1.0, bias=low[:], accum_out=total[:])
            zs[s] = (e, total, 0)

        def invert(s):
            e, total, spare = zs[s]
            inv = work.tile([P, 1], F32, name="inv", bufs=4)
            nc.vector.reciprocal(out=inv[:], in_=total[:])
            zs[s] = (e, inv, 0, 0)

        def weigh(s):
            e, inv, spare, spare = zs.pop(s)
            m = work.tile([P, T], BF16, name="m", bufs=4)
            nc.vector.scalar_tensor_tensor(out=m[:], in0=e[:], scalar=inv[:], in1=gain[:], op0=ALU.mult, op1=ALU.mult)
            ms[s] = m

        def group(s):
            if s >= 30:
                return (s,)
            return (s - 1, s) if s % 2 else ()

        def pack_pe(s):
            if not group(s):
                return
            bank = ps_tr.tile([P, NT * P], F32, name="bank")
            for i, n in enumerate(group(s)):
                words = ms.pop(n)[:].bitcast(F32)
                for u in range(2):
                    nc.tensor.transpose(bank[:, (2 * i + u) * P : (2 * i + u + 1) * P], words[:, u * P : (u + 1) * P], ident[:])
            banks["p", s] = bank

        def pack_copy(s):
            if not group(s):
                return
            bank = banks.pop(("p", s))
            w = len(group(s)) * P
            mt = work.tile([P, 2 * P * NT], BF16, name="mt", align_bytes=64)
            copy = nc.vector.tensor_copy if 0 else nc.scalar.copy
            copy(out=mt[:, 0 : NT * w].bitcast(F32).rearrange("p (n i u) -> p n i u", i=P, u=2), in_=bank[:, 0 : 2 * w].rearrange("p (n u i) -> p n i u", i=P, u=2))
            banks["m", s] = mt

        def pack_quant(s):
            if not group(s):
                return
            mt = banks.pop(("m", s))
            w = len(group(s)) * P
            codes = work.tile([P, 2 * P], U32, name="m_codes", align_bytes=64, bufs=3)
            scl = work.tile([P, 2 * P], U8, name="m_scl", align_bytes=64, bufs=3)
            nc.vector.quantize_mx(out=codes[:, 0:w].bitcast(FP8X4), scales=scl[:, 0:w], in_=mt[:, 0 : NT * w])
            for i, n in enumerate(group(s)):
                mx_m[n] = (codes[:, i * P : (i + 1) * P], scl[:, i * P : (i + 1) * P])

        def widen(s):
            b, t = divmod(s, NT)
            if t == 0:
                v_wide = work.tile([P, NT, E], BF16, name="v_wide")
                vw[b] = v_wide
            code = raw[b][2][:, t * E : (t + 1) * E].bitcast(FP8)
            if 'S' == "S":
                nc.scalar.activation(out=vw[b][:, t, :], in_=code, func=ACT.Copy, scale=vs[:, t : t + 1])
            else:
                nc.vector.tensor_scalar(out=vw[b][:, t, :], in0=code, scalar1=vs[:, t : t + 1], scalar2=None, op0=ALU.mult)
            done.add(("w", s))

        def interleave(s):
            b, h = divmod(s, NT)
            assert ("w", NT * b + 3) in done
            if h == 0:
                v_inter = work.tile([P, E, NT], BF16, name="v_inter", align_bytes=64)
                vi[b] = v_inter
            cols = slice(h * P, (h + 1) * P)
            if 'G' == "G":
                nc.gpsimd.tensor_scalar(out=vi[b][:, cols, :], in0=vw[b][:, :, cols].rearrange("p t n -> p n t"), scalar1=1.0, scalar2=0.0, op0=ALU.mult, op1=ALU.add)
            else:
                nc.vector.tensor_copy(out=vi[b][:, cols, :], in_=vw[b][:, :, cols].rearrange("p t n -> p n t"))
            done.add(("i", s))

        def quant_v(s):
            b, h = divmod(s, NT)
            if h != NT - 1:
                return
            assert ("i", s) in done
            codes = work.tile([P, E], U32, name="v_codes", align_bytes=64)
            scl = work.tile([P, E], U8, name="v_scl", align_bytes=64)
            nc.vector.quantize_mx(out=codes[:].bitcast(FP8X4), scales=scl[:], in_=vi[b][:].rearrange("p n t -> p (n t)"))
            mx_v[b] = (codes, scl)

        def product(s):
            b, it = divmod(s, NT)
            codes, scl = mx_m.pop(s)
            vc, vsc = mx_v[b]
            if s >= 28 and s % 2:
                acc = ps_st.tile([P, E], F32, name="st")
            else:
                acc = ps_pv.tile([P, E], F32, name="acc")
            nc.tensor.matmul_mx(out=acc[:], lhsT=codes.bitcast(FP8X4), lhsT_scale=scl, rhs=vc[:].bitcast(FP8X4), rhs_scale=vsc[:], start=True, stop=True)
            accs[s] = acc

        def leave(s):
            b, it = divmod(s, NT)
            acc = accs.pop(s)
            res = work.tile([P, E], F32, name="res", bufs=4)
            copy = nc.vector.tensor_copy if s in (29, 31) else nc.scalar.copy
            copy(out=res[:], in_=acc[:])
            nc.sync.dma_start(out=out[b, 0, it * P : (it + 1) * P, :], in_=res[:])

        def finish(s):
            product(s)
            leave(s)

        def load_(s):
            if s % NT == 0 and s >= 2 * NT:
                load(s // NT)

        def spread(s):
            if s:
                return
            nc.vector.tensor_scalar(out=g_col[:], in0=g_raw[:], scalar1=math.sqrt(T), scalar2=None, op0=ALU.mult)
            gain_v = gain[:].rearrange("q (u p e) -> q u p e", u=2, e=2)
            for t in range(NT):
                nc.tensor.transpose(gain_v[:, t // 2, :, t % 2], g_col[:, t : t + 1].to_broadcast([P, P]), ident[:])

        step = ((exps, 6), (scores, 0), (invert, 6), (spread, -1), (flatten, 0), (pack_pe, 7), (accum, 1), (interleave, 5), (stencil, 5), (widen, 1), (weigh, 6), (turn_pe, -5), (lowest, 5), (mult, 0), (pack_copy, 7), (turn_copy, -5), (quant_v, 5), (product, 9), (pack_quant, 7), (load_, -8), (leave, 9),)
        tail = ((exps, 6), (scores, 0), (invert, 6), (spread, -2), (flatten, 0), (pack_pe, 7), (accum, 2), (interleave, 5), (stencil, 4), (widen, 1), (weigh, 6), (leave, 10), (lowest, 5), (turn_pe, -4), (mult, 0), (load_, -8), (pack_copy, 7), (turn_copy, -5), (quant_v, 5), (product, 9), (pack_quant, 7),)
        count = {}
        with tc.manual_schedule():
            for s in range(-8, STEPS + 9 + 1):
                for fn, lag in (tail if s >= 33 else step):
                    while count.setdefault(fn, count[leave] if fn is finish else 0) <= s - lag and count[fn] < STEPS:
                        fn(count[fn])
                        count[fn] += 1
